import numpy as np
import ml_dtypes


def mxq(x, axis, fmt="e4m3"):
    dtype, down = {"e4m3": (ml_dtypes.float8_e4m3fn, 7), "e5m2": (ml_dtypes.float8_e5m2, 14)}[fmt]
    v = np.moveaxis(np.asarray(x, np.float32).astype(ml_dtypes.bfloat16).astype(np.float64), axis, -1)
    blocks = v.reshape(v.shape[:-1] + (-1, 32))
    amax = np.abs(blocks).max(-1, keepdims=True)
    byte = np.maximum(np.where(amax > 0, np.frexp(amax)[1] - 1 + 127, 0) - down, 1)
    scale = np.exp2(byte - 127.0)
    codes = (blocks / scale).astype(np.float32).astype(dtype).astype(np.float64)
    return np.moveaxis((codes * scale).reshape(v.shape), -1, axis)


WIDE = False


def mx_kscale(k):
    if not WIDE:
        return np.ones(k)
    levels = np.array([30, -30])
    if k % 512:
        return np.exp2(np.random.permutation(np.resize(levels, k // 32))).repeat(32)
    a = np.empty((k // 512, 16))
    for p in range(k // 512):
        a[p, :8] = np.random.permutation(np.resize(levels, 8))
        for g in range(8):
            far = levels[np.abs(levels - a[p, g]) >= 10]
            a[p, g + 8] = far[np.random.randint(len(far))]
    return np.exp2(a.ravel()).repeat(32)


def f64(x):
    return np.asarray(x).astype(np.float64)


def striped(idx):
    return np.tile(np.asarray(idx).reshape(-1, 16).T, (8, 1)).astype(np.uint16)


def unstriped(offs):
    return offs[:16].T.reshape(-1).astype(np.int64)


E2M1 = np.array([0.0, 0.5, 1.0, 1.5, 2.0, 3.0, 4.0, 6.0, -0.0, -0.5, -1.0, -1.5, -2.0, -3.0, -4.0, -6.0])


def pack_weight(w, fmt):
    k, n = w.shape
    w = f64(np.asarray(w, np.float32).astype(ml_dtypes.bfloat16)).reshape(k // 32, 32, n)
    amax = np.abs(w).max(1)
    if fmt in ("e4m3", "e5m2"):
        byte = np.frexp(amax)[1] - 1 + 127 - (7 if fmt == "e4m3" else 14)
    else:
        mant, ex = np.frexp(amax / 6.0)
        byte = np.where(mant > 0.5, ex, ex - 1) + 127
    byte = np.clip(np.where(amax > 0, byte, 1), 1, 254)
    scaled = (w * np.exp2(127.0 - byte)[:, None, :]).reshape(k, n).astype(np.float32)
    by_word = np.ascontiguousarray(scaled.reshape(k // 512, 128, 4, n).transpose(0, 1, 3, 2))
    if fmt in ("e4m3", "e5m2"):
        words = by_word.astype(ml_dtypes.float8_e4m3fn if fmt == "e4m3" else ml_dtypes.float8_e5m2).view(np.uint8)
    else:
        c = by_word.astype(ml_dtypes.float4_e2m1fn).view(np.uint8) & 0xF
        words = (c[..., 0::2] | (c[..., 1::2] << 4)).reshape(k // 512, 128, 2 * n)
    return np.ascontiguousarray(words), np.ascontiguousarray(byte.astype(np.uint8).reshape(k // 512, 16, n))


def unpack_weight(words, scales, fmt):
    g, _, n = scales.shape
    words = np.ascontiguousarray(words).reshape(g, 128, n, -1)
    if fmt in ("e4m3", "e5m2"):
        vals = words.view(ml_dtypes.float8_e4m3fn if fmt == "e4m3" else ml_dtypes.float8_e5m2).astype(np.float64)
    else:
        nib = np.empty((g, 128, n, 4), np.uint8)
        nib[..., 0::2] = words & 0xF
        nib[..., 1::2] = words >> 4
        vals = E2M1[nib]
    vals = vals * np.repeat(np.exp2(scales.astype(np.float64) - 127.0), 8, axis=1)[..., None]
    return vals.transpose(0, 1, 3, 2).reshape(g * 512, n)


def sigmoid(v):
    return 1.0 / (1.0 + np.exp(-v))


K, T, J, R, O, N, L, E = 512, 2048, 256, 512, 128, 256, 512, 512


def setup_inputs():
    n = np.random.standard_normal
    idx = np.random.permutation(T)[:J]
    idx2 = np.random.permutation(T)[:J]
    idx3 = np.random.permutation(J)[:O]
    idx4 = np.random.permutation(J)[:O]
    idx5 = np.random.permutation(E)[:O]
    fk = mx_kscale(K)
    fr = mx_kscale(R)
    fl = mx_kscale(L)
    xtp = pack_weight(n((K, T)) / fk[:, None], "e4m3")
    wp = pack_weight(n((K, R)) * 1 / np.sqrt(K) * fk[:, None], "e2m1")
    w2p = pack_weight(n((K, R)) * 1 / np.sqrt(K) * fk[:, None] * fr, "e5m2")
    wbp = pack_weight(n((R, N)) * 1 / np.sqrt(R) / fr[:, None], "e5m2")
    sxp = pack_weight(n((L, O)) / fl[:, None], "e2m1")
    wsp = pack_weight(n((L, N)) * 1 / np.sqrt(L) * fl[:, None], "e5m2")
    return {
        "xt_words": xtp[0],
        "xt_scales": xtp[1],
        "w_words": wp[0],
        "w_scales": wp[1],
        "w2_words": w2p[0],
        "w2_scales": w2p[1],
        "sg": (np.random.uniform(0.6, 1.6, (R, 1))).astype(np.float32),
        "wb_words": wbp[0],
        "wb_scales": wbp[1],
        "sx_words": sxp[0],
        "sx_scales": sxp[1],
        "ws_words": wsp[0],
        "ws_scales": wsp[1],
        "tz": (n((N, E))).astype(np.float32),
        "so": (np.random.uniform(0.6, 1.6, (N, 1))).astype(np.float32),
        "bo": (np.random.uniform(-1.0, 1.0, (N, 1))).astype(np.float32),
        "offs": striped(idx),
        "offs2": striped(idx2),
        "offs3": striped(idx3),
        "offs4": striped(idx4),
        "offs5": striped(idx5),
    }


def reference(xt_words, xt_scales, w_words, w_scales, w2_words, w2_scales, sg, wb_words, wb_scales, sx_words, sx_scales, ws_words, ws_scales, tz, so, bo, offs, offs2, offs3, offs4, offs5):
    idx = unstriped(offs)
    idx2 = unstriped(offs2)
    idx3 = unstriped(offs3)
    idx4 = unstriped(offs4)
    idx5 = unstriped(offs5)
    xtu = unpack_weight(xt_words, xt_scales, "e4m3")
    wu = unpack_weight(w_words, w_scales, "e2m1")
    w2u = unpack_weight(w2_words, w2_scales, "e5m2")
    wbu = unpack_weight(wb_words, wb_scales, "e5m2")
    sxu = unpack_weight(sx_words, sx_scales, "e2m1")
    wsu = unpack_weight(ws_words, ws_scales, "e5m2")
    xtidxg = xtu[:, idx]
    a = wu.T @ xtidxg
    xtidx2g = xtu[:, idx2]
    b = w2u.T @ xtidx2g
    hid = np.maximum(b[:, idx3], b[:, idx4]) * sigmoid(a[:, idx4] * f64(sg))
    hidq = mxq(hid, 0, "e4m3")
    p = wbu.T @ hidq + wsu.T @ sxu
    y = p * sigmoid(f64(tz)[:, idx5] * f64(so) + f64(bo))
    return y

@@ -1,0 +1,198 @@
+from contextlib import ExitStack
+
+import concourse.mybir as mybir
+
+K, T, J, R, O, N, L, E = 512, 2048, 256, 512, 128, 256, 512, 512
+FLOPS = 2 * (2 * K * R * J + R * N * O + L * N * O)
+
+F32 = mybir.dt.float32
+BF16 = mybir.dt.bfloat16
+I32 = mybir.dt.int32
+U32 = mybir.dt.uint32
+U16 = mybir.dt.uint16
+U8 = mybir.dt.uint8
+E4M3 = mybir.dt.float8_e4m3fn_x4
+E5M2 = mybir.dt.float8_e5m2_x4
+E2M1 = mybir.dt.float4_e2m1fn_x4
+ALU = mybir.AluOpType
+ACT = mybir.ActivationFunctionType
+
+P = 128
+PACK = 4
+
+
+def tile_list_ahead_agree_skip_finalgate_kernel(
+    tc, xt_words, xt_scales, w_words, w_scales, w2_words, w2_scales, sg, wb_words, wb_scales,
+    sx_words, sx_scales, ws_words, ws_scales, tz, so, bo, offs, offs2, offs3, offs4, offs5, out,
+):
+    nc = tc.nc
+    with ExitStack() as ctx:
+        pool = ctx.enter_context(tc.tile_pool(name="sbuf", bufs=1))
+        shared = ctx.enter_context(tc.tile_pool(name="shared", bufs=1))
+        psum = ctx.enter_context(tc.psum_pool(name="psum", bufs=1))
+
+        def tile(shape, dtype, name):
+            return pool.tile(shape, dtype, name=name, align_bytes=64)
+
+        def placed(shape, dtype, name, offset):
+            return shared.tile(shape, dtype, name=name, align_bytes=64, offset=offset)
+
+        def clear_other_rows(dst):
+            nc.vector.memset(dst[0:112, :].bitcast(I32), 0)
+
+        def words_of(dram):
+            return dram[0].rearrange("p c r -> p (c r)").bitcast(I32)
+
+        def load_rows(queue, dst, dram):
+            queue.dma_start(out=dst.bitcast(I32), in_=dram[0].bitcast(I32))
+
+        def spread_rows(plane, row):
+            for q in range(4):
+                if 32 * q != row + 4 * q:
+                    nc.sync.dma_start(
+                        out=plane[32 * q : 32 * q + 4, :].bitcast(I32),
+                        in_=plane[row + 4 * q : row + 4 * q + 4, :].bitcast(I32),
+                    )
+
+        list2 = tile([P, J // 16], U16, "list2")
+        list1 = tile([P, J // 16], U16, "list1")
+        nc.sync.dma_start(list2[:], offs2)
+        nc.sync.dma_start(list1[:], offs)
+
+        xs = tile([P, T], U8, "xs")
+        raw_s = tile([P, 2 * R], U8, "raw_s")
+        load_rows(nc.scalar, xs[112:128, :], xt_scales)
+        load_rows(nc.scalar, raw_s[112:128, 0:R], w2_scales)
+        load_rows(nc.scalar, raw_s[112:128, R:], w_scales)
+        clear_other_rows(xs)
+        clear_other_rows(raw_s)
+
+        sg_t = tile([P, PACK], F32, "sg_t")
+        so_t = tile([P, 2], F32, "so_t")
+        bo_t = tile([P, 2], F32, "bo_t")
+        nc.gpsimd.dma_start(out=sg_t[:], in_=sg.rearrange("(p t) o -> p (t o)", t=PACK))
+        with nc.allow_non_contiguous_dma(reason="one value a partition"):
+            nc.gpsimd.dma_start(out=so_t[:], in_=so.rearrange("(h p) o -> p (h o)", h=2))
+            nc.gpsimd.dma_start(out=bo_t[:], in_=bo.rearrange("(h p) o -> p (h o)", h=2))
+
+        raw_w = placed([P, 6 * R], U8, "raw_w", 0)
+        w2_raw = raw_w[:, 0 : 4 * R].bitcast(I32)
+        w_raw = raw_w[:, 4 * R : 6 * R]
+        xw = placed([P, T], I32, "xw", 6 * R)
+        nc.sync.dma_start(out=w2_raw, in_=words_of(w2_words))
+        nc.sync.dma_start(out=w_raw.bitcast(I32), in_=w_words[0].bitcast(I32))
+        nc.sync.dma_start(out=xw[:], in_=words_of(xt_words))
+
+        xg_s = tile([P, J], U8, "xg_s")
+        plane_b = tile([P, J + R], U8, "plane_b")
+        plane_a = tile([P, J + R], U8, "plane_a")
+        for g, (picks, plane) in enumerate(((list2, plane_b), (list1, plane_a))):
+            nc.vector.tensor_copy(xg_s[:], xs[:].indirect(picks[:]))
+            nc.vector.tensor_copy(
+                out=plane[:, J:].rearrange("p (t c i) -> p c t i", t=PACK, i=16),
+                in_=raw_s[:, g * R : (g + 1) * R].rearrange("p (c i t) -> p c t i", t=PACK, i=16),
+            )
+            nc.vector.tensor_copy(out=plane[:, 0:J].bitcast(I32), in_=xg_s[:].bitcast(I32))
+            spread_rows(plane, 112)
+
+        w2_p = tile([P, R], I32, "w2_p")
+        w_p = tile([P, 2 * R], U8, "w_p")
+        nc.scalar.copy(
+            out=w2_p[:].bitcast(U32).rearrange("p (t c i) -> p c t i", t=PACK, i=4),
+            in_=w2_raw.bitcast(U32).rearrange("p (c i t) -> p c t i", t=PACK, i=4),
+        )
+        nc.scalar.copy(
+            out=w_p[:].bitcast(U16).rearrange("p (t c i) -> p c t i", t=PACK, i=8),
+            in_=w_raw.bitcast(U16).rearrange("p (c i t) -> p c t i", t=PACK, i=8),
+        )
+        xg2 = tile([P, J], U32, "xg2")
+        xg1 = tile([P, J], U32, "xg1")
+        nc.vector.tensor_copy(xg2[:], xw[:].bitcast(U32).indirect(list2[:]))
+        nc.vector.tensor_copy(xg1[:], xw[:].bitcast(U32).indirect(list1[:]))
+
+        list3 = tile([P, O // 16], U16, "list3")
+        list4 = tile([P, O // 16], U16, "list4")
+        list5 = tile([P, O // 16], U16, "list5")
+        nc.sync.dma_start(list3[:], offs3)
+        nc.sync.dma_start(list4[:], offs4)
+        nc.sync.dma_start(list5[:], offs5)
+        plane2 = placed([P, 2 * N + O], U8, "plane2", 0)
+        nc.gpsimd.memset(plane2[:].bitcast(I32), 0)
+        load_rows(nc.sync, plane2[0:16, 0:N], wb_scales)
+        load_rows(nc.sync, plane2[0:16, N : 2 * N], ws_scales)
+        load_rows(nc.sync, plane2[0:16, 2 * N :], sx_scales)
+        ws_w = placed([P, N], I32, "ws_w", 1024)
+        sx_w = placed([P, 2 * O], U8, "sx_w", 704)
+        wb_w = placed([P, N], I32, "wb_w", 2048)
+        nc.sync.dma_start(out=ws_w[:], in_=words_of(ws_words))
+        nc.sync.dma_start(out=sx_w[:].bitcast(I32), in_=sx_words[0].bitcast(I32))
+        nc.sync.dma_start(out=wb_w[:], in_=words_of(wb_words))
+        tz_t = [placed([P, E], F32, "tz%d" % h, 6 * R + 4 * E * h) for h in range(2)]
+        for h in range(2):
+            nc.sync.dma_start(out=tz_t[h][:], in_=tz[h * P : (h + 1) * P, :])
+        spread_rows(plane2, 0)
+
+        b_sb = [tile([P, J], F32, "b_sb%d" % t) for t in range(PACK)]
+        a_sb = [tile([P, J], F32, "a_sb%d" % t) for t in range(PACK)]
+        g3 = tile([P, PACK, O], F32, "g3")
+        g4 = tile([P, PACK, O], F32, "g4")
+        gate = tile([P, PACK, O], F32, "gate")
+        big = tile([P, PACK, O], F32, "big")
+        for t in range(PACK):
+            b_ps = psum.tile([P, J], F32, name="b_ps%d" % t, tag="bank%d" % t)
+            nc.tensor.matmul_mx(
+                out=b_ps[:], lhsT=w2_p[:, t * P : (t + 1) * P].bitcast(E5M2),
+                lhsT_scale=plane_b[:, J + t * P : J + (t + 1) * P],
+                rhs=xg2[:].bitcast(E4M3), rhs_scale=plane_b[:, 0:J], start=True, stop=True,
+            )
+            nc.scalar.copy(out=b_sb[t][:], in_=b_ps[:])
+            nc.vector.tensor_copy(g3[:, t, :], b_sb[t][:].indirect(list3[:]))
+            nc.vector.tensor_copy(g4[:, t, :], b_sb[t][:].indirect(list4[:]))
+            if t % 2 == 1:
+                nc.vector.tensor_tensor(big[:, t - 1 : t + 1, :], g3[:, t - 1 : t + 1, :], g4[:, t - 1 : t + 1, :], ALU.max)
+        for t in range(PACK):
+            a_ps = psum.tile([P, J], F32, name="a_ps%d" % t, tag="bank%d" % ((4 + t) % 6))
+            nc.tensor.matmul_mx(
+                out=a_ps[:], lhsT=w_p[:, 2 * t * P : 2 * (t + 1) * P].bitcast(E2M1),
+                lhsT_scale=plane_a[:, J + t * P : J + (t + 1) * P],
+                rhs=xg1[:].bitcast(E4M3), rhs_scale=plane_a[:, 0:J], start=True, stop=True,
+            )
+            nc.scalar.copy(out=a_sb[t][:], in_=a_ps[:])
+            nc.scalar.activation(out=gate[:, t, :], in_=a_sb[t][:].indirect(list4[:]), func=ACT.Sigmoid, scale=sg_t[:, t : t + 1])
+
+        hid = tile([P, O * PACK], BF16, "hid")
+        nc.vector.tensor_tensor(
+            hid[:].rearrange("p (c i t) -> p c t i", t=PACK, i=4),
+            big[:].rearrange("p t (c i) -> p c t i", i=4),
+            gate[:].rearrange("p t (c i) -> p c t i", i=4),
+            ALU.mult,
+        )
+        hid_w = tile([P, O], U32, "hid_w")
+        hid_s = tile([P, O], U8, "hid_s")
+        nc.vector.quantize_mx(out=hid_w[:].bitcast(E4M3), scales=hid_s[:], in_=hid[:])
+
+        last = tile([P, 2, O], F32, "last")
+        for h in range(2):
+            nc.scalar.activation(
+                out=last[:, h, :], in_=tz_t[h][:].indirect(list5[:]), func=ACT.Sigmoid,
+                scale=so_t[:, h : h + 1], bias=bo_t[:, h : h + 1],
+            )
+
+        p_ps = [psum.tile([P, O], F32, name="p_ps%d" % h, tag="bank%d" % (6 + h)) for h in range(2)]
+        for h in range(2):
+            nc.tensor.matmul_mx(
+                out=p_ps[h][:], lhsT=ws_w[:, h * P : (h + 1) * P].bitcast(E5M2),
+                lhsT_scale=plane2[:, N + h * P : N + (h + 1) * P],
+                rhs=sx_w[:].bitcast(E2M1), rhs_scale=plane2[:, 2 * N : 2 * N + O], start=True, stop=False,
+            )
+        for h in range(2):
+            nc.tensor.matmul_mx(
+                out=p_ps[h][:], lhsT=wb_w[:, h * P : (h + 1) * P].bitcast(E5M2),
+                lhsT_scale=plane2[:, h * P : (h + 1) * P],
+                rhs=hid_w[:].bitcast(E4M3), rhs_scale=hid_s[:], start=False, stop=True,
+            )
+        queues = (nc.sync, nc.scalar)
+        for h in range(2):
+            y = tile([P, O], F32, "y%d" % h)
+            nc.vector.tensor_tensor(y[:], p_ps[h][:], last[:, h, :], ALU.mult)
+            queues[h].dma_start(out=out[h * P : (h + 1) * P, :], in_=y[:])

@@ -75,6 +75,11 @@ def tile_list_ahead_agree_skip_finalgate_kernel(
             nc.gpsimd.dma_start(out=so_t[:], in_=so.rearrange("(h p) o -> p (h o)", h=2))
             nc.gpsimd.dma_start(out=bo_t[:], in_=bo.rearrange("(h p) o -> p (h o)", h=2))
 
+        warm_in = tile([P, 1], F32, "warm_in")
+        warm_out = tile([P, 1], F32, "warm_out")
+        nc.vector.memset(warm_in[:], 0.0)
+        nc.scalar.activation(out=warm_out[:], in_=warm_in[:], func=ACT.Sigmoid)
+
         raw_w = placed([P, 6 * R], U8, "raw_w", 0)
         w2_raw = raw_w[:, 0 : 4 * R].bitcast(I32)
         w_raw = raw_w[:, 4 * R : 6 * R]

from contextlib import ExitStack

import concourse.mybir as mybir

K, T, J, R, O, N, L, E = 512, 2048, 256, 512, 128, 256, 512, 512
FLOPS = 2 * (2 * K * R * J + R * N * O + L * N * O)

F32 = mybir.dt.float32
BF16 = mybir.dt.bfloat16
I32 = mybir.dt.int32
U32 = mybir.dt.uint32
U16 = mybir.dt.uint16
U8 = mybir.dt.uint8
E4M3 = mybir.dt.float8_e4m3fn_x4
E5M2 = mybir.dt.float8_e5m2_x4
E2M1 = mybir.dt.float4_e2m1fn_x4
ALU = mybir.AluOpType
ACT = mybir.ActivationFunctionType

P = 128
PACK = 4


def tile_list_ahead_agree_skip_finalgate_kernel(
    tc, xt_words, xt_scales, w_words, w_scales, w2_words, w2_scales, sg, wb_words, wb_scales,
    sx_words, sx_scales, ws_words, ws_scales, tz, so, bo, offs, offs2, offs3, offs4, offs5, out,
):
    nc = tc.nc
    with ExitStack() as ctx:
        pool = ctx.enter_context(tc.tile_pool(name="sbuf", bufs=1))
        shared = ctx.enter_context(tc.tile_pool(name="shared", bufs=1))
        psum = ctx.enter_context(tc.psum_pool(name="psum", bufs=1))

        def tile(shape, dtype, name):
            return pool.tile(shape, dtype, name=name, align_bytes=64)

        def placed(shape, dtype, name, offset):
            return shared.tile(shape, dtype, name=name, align_bytes=64, offset=offset)

        def clear_other_rows(dst):
            nc.vector.memset(dst[0:112, :].bitcast(I32), 0)

        def words_of(dram):
            return dram[0].rearrange("p c r -> p (c r)").bitcast(I32)

        def load_rows(queue, dst, dram):
            queue.dma_start(out=dst.bitcast(I32), in_=dram[0].bitcast(I32))

        def spread_rows(plane, row):
            for q in range(4):
                if 32 * q != row + 4 * q:
                    nc.sync.dma_start(
                        out=plane[32 * q : 32 * q + 4, :].bitcast(I32),
                        in_=plane[row + 4 * q : row + 4 * q + 4, :].bitcast(I32),
                    )

        list2 = tile([P, J // 16], U16, "list2")
        list1 = tile([P, J // 16], U16, "list1")
        nc.sync.dma_start(list2[:], offs2)
        nc.sync.dma_start(list1[:], offs)

        xs = tile([P, T], U8, "xs")
        raw_s = tile([P, 2 * R], U8, "raw_s")
        load_rows(nc.scalar, xs[112:128, :], xt_scales)
        load_rows(nc.scalar, raw_s[112:128, 0:R], w2_scales)
        load_rows(nc.scalar, raw_s[112:128, R:], w_scales)
        clear_other_rows(xs)
        clear_other_rows(raw_s)

        sg_t = tile([P, PACK], F32, "sg_t")
        so_t = tile([P, 2], F32, "so_t")
        bo_t = tile([P, 2], F32, "bo_t")
        nc.gpsimd.dma_start(out=sg_t[:], in_=sg.rearrange("(p t) o -> p (t o)", t=PACK))
        with nc.allow_non_contiguous_dma(reason="one value a partition"):
            nc.gpsimd.dma_start(out=so_t[:], in_=so.rearrange("(h p) o -> p (h o)", h=2))
            nc.gpsimd.dma_start(out=bo_t[:], in_=bo.rearrange("(h p) o -> p (h o)", h=2))

        warm_in = tile([P, 1], F32, "warm_in")
        warm_out = tile([P, 1], F32, "warm_out")
        nc.vector.memset(warm_in[:], 0.0)
        nc.scalar.activation(out=warm_out[:], in_=warm_in[:], func=ACT.Sigmoid)

        raw_w = placed([P, 6 * R], U8, "raw_w", 0)
        w2_raw = raw_w[:, 0 : 4 * R].bitcast(I32)
        w_raw = raw_w[:, 4 * R : 6 * R]
        xw = placed([P, T], I32, "xw", 6 * R)
        nc.sync.dma_start(out=w2_raw, in_=words_of(w2_words))
        nc.sync.dma_start(out=w_raw.bitcast(I32), in_=w_words[0].bitcast(I32))
        nc.sync.dma_start(out=xw[:], in_=words_of(xt_words))

        xg_s = tile([P, J], U8, "xg_s")
        plane_b = tile([P, J + R], U8, "plane_b")
        plane_a = tile([P, J + R], U8, "plane_a")
        for g, (picks, plane) in enumerate(((list2, plane_b), (list1, plane_a))):
            nc.vector.tensor_copy(xg_s[:], xs[:].indirect(picks[:]))
            nc.vector.tensor_copy(
                out=plane[:, J:].rearrange("p (t c i) -> p c t i", t=PACK, i=16),
                in_=raw_s[:, g * R : (g + 1) * R].rearrange("p (c i t) -> p c t i", t=PACK, i=16),
            )
            nc.vector.tensor_copy(out=plane[:, 0:J].bitcast(I32), in_=xg_s[:].bitcast(I32))
            spread_rows(plane, 112)

        w2_p = tile([P, R], I32, "w2_p")
        w_p = tile([P, 2 * R], U8, "w_p")
        nc.scalar.copy(
            out=w2_p[:].bitcast(U32).rearrange("p (t c i) -> p c t i", t=PACK, i=4),
            in_=w2_raw.bitcast(U32).rearrange("p (c i t) -> p c t i", t=PACK, i=4),
        )
        nc.scalar.copy(
            out=w_p[:].bitcast(U16).rearrange("p (t c i) -> p c t i", t=PACK, i=8),
            in_=w_raw.bitcast(U16).rearrange("p (c i t) -> p c t i", t=PACK, i=8),
        )
        xg2 = tile([P, J], U32, "xg2")
        xg1 = tile([P, J], U32, "xg1")
        nc.vector.tensor_copy(xg2[:], xw[:].bitcast(U32).indirect(list2[:]))
        nc.vector.tensor_copy(xg1[:], xw[:].bitcast(U32).indirect(list1[:]))

        list3 = tile([P, O // 16], U16, "list3")
        list4 = tile([P, O // 16], U16, "list4")
        list5 = tile([P, O // 16], U16, "list5")
        nc.sync.dma_start(list3[:], offs3)
        nc.sync.dma_start(list4[:], offs4)
        nc.sync.dma_start(list5[:], offs5)
        plane2 = placed([P, 2 * N + O], U8, "plane2", 0)
        nc.gpsimd.memset(plane2[:].bitcast(I32), 0)
        load_rows(nc.sync, plane2[0:16, 0:N], wb_scales)
        load_rows(nc.sync, plane2[0:16, N : 2 * N], ws_scales)
        load_rows(nc.sync, plane2[0:16, 2 * N :], sx_scales)
        ws_w = placed([P, N], I32, "ws_w", 1024)
        sx_w = placed([P, 2 * O], U8, "sx_w", 704)
        wb_w = placed([P, N], I32, "wb_w", 2048)
        nc.sync.dma_start(out=ws_w[:], in_=words_of(ws_words))
        nc.sync.dma_start(out=sx_w[:].bitcast(I32), in_=sx_words[0].bitcast(I32))
        nc.sync.dma_start(out=wb_w[:], in_=words_of(wb_words))
        tz_t = [placed([P, E], F32, "tz%d" % h, 6 * R + 4 * E * h) for h in range(2)]
        for h in range(2):
            nc.sync.dma_start(out=tz_t[h][:], in_=tz[h * P : (h + 1) * P, :])
        spread_rows(plane2, 0)

        b_sb = [tile([P, J], F32, "b_sb%d" % t) for t in range(PACK)]
        a_sb = [tile([P, J], F32, "a_sb%d" % t) for t in range(PACK)]
        g3 = tile([P, PACK, O], F32, "g3")
        g4 = tile([P, PACK, O], F32, "g4")
        gate = tile([P, PACK, O], F32, "gate")
        big = tile([P, PACK, O], F32, "big")
        for t in range(PACK):
            b_ps = psum.tile([P, J], F32, name="b_ps%d" % t, tag="bank%d" % t)
            nc.tensor.matmul_mx(
                out=b_ps[:], lhsT=w2_p[:, t * P : (t + 1) * P].bitcast(E5M2),
                lhsT_scale=plane_b[:, J + t * P : J + (t + 1) * P],
                rhs=xg2[:].bitcast(E4M3), rhs_scale=plane_b[:, 0:J], start=True, stop=True,
            )
            nc.scalar.copy(out=b_sb[t][:], in_=b_ps[:])
            nc.vector.tensor_copy(g3[:, t, :], b_sb[t][:].indirect(list3[:]))
            nc.vector.tensor_copy(g4[:, t, :], b_sb[t][:].indirect(list4[:]))
            if t % 2 == 1:
                nc.vector.tensor_tensor(big[:, t - 1 : t + 1, :], g3[:, t - 1 : t + 1, :], g4[:, t - 1 : t + 1, :], ALU.max)
        for t in range(PACK):
            a_ps = psum.tile([P, J], F32, name="a_ps%d" % t, tag="bank%d" % ((4 + t) % 6))
            nc.tensor.matmul_mx(
                out=a_ps[:], lhsT=w_p[:, 2 * t * P : 2 * (t + 1) * P].bitcast(E2M1),
                lhsT_scale=plane_a[:, J + t * P : J + (t + 1) * P],
                rhs=xg1[:].bitcast(E4M3), rhs_scale=plane_a[:, 0:J], start=True, stop=True,
            )
            nc.scalar.copy(out=a_sb[t][:], in_=a_ps[:])
            nc.scalar.activation(out=gate[:, t, :], in_=a_sb[t][:].indirect(list4[:]), func=ACT.Sigmoid, scale=sg_t[:, t : t + 1])

        hid = tile([P, O * PACK], BF16, "hid")
        nc.vector.tensor_tensor(
            hid[:].rearrange("p (c i t) -> p c t i", t=PACK, i=4),
            big[:].rearrange("p t (c i) -> p c t i", i=4),
            gate[:].rearrange("p t (c i) -> p c t i", i=4),
            ALU.mult,
        )
        hid_w = tile([P, O], U32, "hid_w")
        hid_s = tile([P, O], U8, "hid_s")
        nc.vector.quantize_mx(out=hid_w[:].bitcast(E4M3), scales=hid_s[:], in_=hid[:])

        last = tile([P, 2, O], F32, "last")
        for h in range(2):
            nc.scalar.activation(
                out=last[:, h, :], in_=tz_t[h][:].indirect(list5[:]), func=ACT.Sigmoid,
                scale=so_t[:, h : h + 1], bias=bo_t[:, h : h + 1],
            )

        p_ps = [psum.tile([P, O], F32, name="p_ps%d" % h, tag="bank%d" % (6 + h)) for h in range(2)]
        for h in range(2):
            nc.tensor.matmul_mx(
                out=p_ps[h][:], lhsT=ws_w[:, h * P : (h + 1) * P].bitcast(E5M2),
                lhsT_scale=plane2[:, N + h * P : N + (h + 1) * P],
                rhs=sx_w[:].bitcast(E2M1), rhs_scale=plane2[:, 2 * N : 2 * N + O], start=True, stop=False,
            )
        for h in range(2):
            nc.tensor.matmul_mx(
                out=p_ps[h][:], lhsT=wb_w[:, h * P : (h + 1) * P].bitcast(E5M2),
                lhsT_scale=plane2[:, h * P : (h + 1) * P],
                rhs=hid_w[:].bitcast(E4M3), rhs_scale=hid_s[:], start=False, stop=True,
            )
        queues = (nc.sync, nc.scalar)
        for h in range(2):
            y = tile([P, O], F32, "y%d" % h)
            nc.vector.tensor_tensor(y[:], p_ps[h][:], last[:, h, :], ALU.mult)
            queues[h].dma_start(out=out[h * P : (h + 1) * P, :], in_=y[:])
